import numpy as np, ml_dtypes
CORES = [1,2,5,6,9,10,13,14,17,18,21,22,25,26,29,30]
N = 16
F = 256
def setup_inputs(rng):
    return {"a": rng.standard_normal((N, 128, N * 128), dtype=np.float32).astype(ml_dtypes.bfloat16), "w": rng.standard_normal((N, 128, F), dtype=np.float32).astype(ml_dtypes.bfloat16)}
def reference(a, w):
    tot = np.zeros((N * 128, F))
    for j in range(N):
        tot += a[j].astype(np.float64).T @ w[j].astype(np.float64)
    return {"y": np.stack([tot[128 * r:128 * r + 128] for r in range(N)]).astype(ml_dtypes.bfloat16 if a.dtype != np.float64 else np.float64)}

@@ -1,0 +1,216 @@
+from concourse.bass import DstId, RemoteDMATransfer
+from concourse.mybir import AluOpType
+
+F = 256
+KINDS = ["far", "mate", "plane", "own"]
+
+SCRATCH = {
+    "a_sb": ("sbuf", [128, 2048], "bfloat16"),
+    "w_sb": ("sbuf", [128, F], "bfloat16"),
+    "w_in": ("sbuf", [128, 3 * F], "bfloat16"),
+    "a_in": ("sbuf", [128, 3 * 2 * F], "bfloat16"),
+    "out_sb": ("sbuf", [128, 4 * F], "bfloat16"),
+    "rx": ("sbuf", [128, 4 * F], "bfloat16"),
+    "y_sb": ("sbuf", [128, F], "bfloat16"),
+    "ps0": ("psum", [128, 512], "float32"),
+    "ps1": ("psum", [128, 512], "float32"),
+    "ps2": ("psum", [128, 512], "float32"),
+    "ps3": ("psum", [128, 512], "float32"),
+    "acc0": ("psum", [128, 512], "float32"),
+    "acc1": ("psum", [128, 512], "float32"),
+}
+SEMAPHORES = ["ld_far", "ld_mate", "ld_plane", "ld_own", "in1", "in2",
+              "mm0", "mm1", "mm2", "mm3", "cp0", "cp1", "cp2", "cp3",
+              "arr_far", "arr_mate", "arr_plane", "arr_own", "vs", "fin", "st", "sent"]
+
+
+def _bits(mask):
+    return [1 << b for b in range(mask.bit_length()) if (mask >> b) & 1]
+
+
+def _shares(n_items, n_engines):
+    if n_items == 3:
+        return [n_engines // 2, n_engines // 4, n_engines // 4]
+    return [n_engines // n_items] * n_items
+
+
+def rank_program(g, core, T, topo):
+    if T.rank_of(core) is None:
+        return
+    cores = list(T.cores)
+    sem = T.sem
+    chips = sorted({topo.chip(k) for k in cores})
+
+    def kind(c, x):
+        if x == c:
+            return "own"
+        if topo.mates(c, x):
+            return "mate"
+        if topo.same_plane(c, x):
+            return "plane"
+        return "far"
+
+    def chip_of_kind(c, kd):
+        return [x for x in chips if kind(c, x) == kd][0]
+
+    def ranks_on(c, die=None):
+        return [k for k in cores if topo.chip(k) == c and (die is None or topo.die(k) == die)]
+
+    def is_port(k):
+        return all(topo.may_write(k, d) for d in cores if d != k)
+
+    def kinds_of(k):
+        return ("far", "mate") if is_port(k) else ("plane", "own")
+
+    def owners(k, kd):
+        return ranks_on(chip_of_kind(topo.chip(k), kd), topo.die(k))
+
+    def reducer(c, kd, die):
+        return [k for k in ranks_on(c, die) if kd in kinds_of(k)][0]
+
+    def exchange(k):
+        rest = [d for d in ranks_on(topo.chip(k)) if d != k]
+        ports = [d for d in rest if is_port(d)]
+        plain = [d for d in rest if not is_port(d)]
+        if is_port(k):
+            calls = [[(ports[0], "w"), (ports[0], 0)],
+                     [(ports[0], 1), (plain[0], "w"), (plain[1], "w")],
+                     [(plain[0], 0), (plain[1], 0), (plain[0], 1), (plain[1], 1)]]
+        else:
+            calls = [[(ports[0], "w"), (ports[1], "w"), (ports[0], 0), (ports[1], 0)],
+                     [(ports[0], 1), (ports[1], 1), (plain[0], "w"), (plain[0], 0)],
+                     [(plain[0], 1)]]
+        out = []
+        for call in calls:
+            n = min(len(_bits(topo.mask(k, d))) for d, _ in call)
+            out.append([(d, what, e) for (d, what), e in zip(call, _shares(len(call), n))])
+        return out
+
+    chip = topo.chip(core)
+    mine = ranks_on(chip)
+    my_kinds = kinds_of(core)
+    sent = [0]
+
+    def issue(items):
+        pool = None
+        for d, _, _, _, _ in items:
+            m = topo.mask(core, d)
+            pool = m if pool is None else pool & m
+        pool = _bits(pool)
+        trs, i = [], 0
+        for d, dap, sap, rs, e in items:
+            rid, pid, _ = topo.addr(d)
+            trs.append((rid, pid, sum(pool[i:i + e]), dap, sap, rs))
+            i += e
+            sent[0] += e
+        if len(trs) == 1:
+            rid, pid, m, dap, sap, rs = trs[0]
+            g.remote_dma(dap, sap, rs, sem.sent, pid, rid, m)
+        else:
+            g.remote_dma_fused([RemoteDMATransfer(dst_ids=[DstId(rid=rid, pnc=pid)], dma_engine_mask=m,
+                                                  remote_sem=rs, src=sap, dst=dap)
+                                for rid, pid, m, dap, sap, rs in trs], local_sem=sem.sent)
+
+    def col(k):
+        return 128 * T.rank_of(k)
+
+    ld_total = {kd: 16 for kd in KINDS}
+    ld_total["far"] = 32
+    g.sync.dma_start(T.w_sb[:], T.w[:]).then_inc(sem.ld_far, 16)
+    for n, kd in enumerate(KINDS):
+        c0 = min(col(k) for k in ranks_on(chip_of_kind(chip, kd)))
+        q = g.scalar if n % 2 == 0 else g.sync
+        q.dma_start(T.a_sb[:, c0:c0 + 2 * F], T.a[:, c0:c0 + 2 * F]).then_inc(sem["ld_" + kd], 16)
+
+    waited = set()
+    for call in exchange(core):
+        items = []
+        for d, what, e in call:
+            slot = [k for k in mine if k != d].index(core)
+            if what == "w":
+                need, sap, dap, rs = "far", T.w_sb[:], T.w_in[:, F * slot:F * slot + F], sem.in1
+            else:
+                need = kinds_of(d)[what]
+                c0 = min(col(o) for o in owners(d, need))
+                sap = T.a_sb[:, c0:c0 + F]
+                dap = T.a_in[:, 2 * F * slot + F * what:2 * F * slot + F * what + F]
+                rs = sem.in1 if what == 0 else sem.in2
+            if need not in waited:
+                waited.add(need)
+                g.wait_ge(sem["ld_" + need], ld_total[need])
+            items.append((d, dap, sap, rs, e))
+        issue(items)
+
+    in_total = [0, 0]
+    for k in mine:
+        if k != core:
+            for call in exchange(k):
+                for d, what, e in call:
+                    if d == core:
+                        in_total[1 if what == 1 else 0] += e
+
+    blocks = [o for kd in my_kinds for o in owners(core, kd)]
+    ps = [T.ps0, T.ps1, T.ps2, T.ps3]
+    te = g.tensor
+    te.wait_ge(sem.ld_far, ld_total["far"])
+    for kd in my_kinds:
+        if kd != "far":
+            te.wait_ge(sem["ld_" + kd], ld_total[kd])
+    for b, o in enumerate(blocks):
+        te.matmul(ps[b][:, 0:F], T.a_sb[:, col(o):col(o) + 128], T.w_sb[:], True, False)
+    for half in range(2):
+        te.wait_ge(sem.in1 if half == 0 else sem.in2, in_total[half])
+        for b in (2 * half, 2 * half + 1):
+            for s in range(3):
+                mm = te.matmul(ps[b][:, 0:F], T.a_in[:, 2 * F * s + 128 * b:2 * F * s + 128 * b + 128],
+                               T.w_in[:, F * s:F * s + F], False, s == 2)
+            mm.then_inc(sem["mm%d" % b], 1)
+
+    ve = g.vector
+    for b, o in enumerate(blocks):
+        if o != core:
+            ve.wait_ge(sem["mm%d" % b], 1)
+            ve.tensor_copy(T.out_sb[:, F * b:F * b + F], ps[b][:, 0:F]).then_inc(sem["cp%d" % b], 1)
+    for half, kd in enumerate(my_kinds):
+        slot = KINDS.index(kd)
+        items = []
+        todo = [b for b in (2 * half, 2 * half + 1) if blocks[b] != core]
+        for b in todo:
+            g.wait_ge(sem["cp%d" % b], 1)
+            e = len(_bits(topo.mask(core, blocks[b]))) // len(todo)
+            items.append((blocks[b], T.rx[:, F * slot:F * slot + F], T.out_sb[:, F * b:F * b + F],
+                          sem["arr_" + kd], e))
+        issue(items)
+
+    def arrival(kd):
+        s = reducer(chip_of_kind(chip, kd), kd, topo.die(core))
+        n = len([o for o in owners(s, kd) if o != s])
+        return len(_bits(topo.mask(s, core))) // n
+
+    def rx(kd):
+        slot = KINDS.index(kd)
+        return T.rx[:, F * slot:F * slot + F]
+
+    if core in blocks:
+        b = blocks.index(core)
+        ve.wait_ge(sem["mm%d" % b], 1)
+        terms = [ps[b][:, 0:F]] + [rx(kd) for kd in ("far", "mate", "plane")]
+        waits = [None, "far", "mate", "plane"]
+    else:
+        terms = [rx(kd) for kd in KINDS]
+        waits = list(KINDS)
+    outs = [T.acc0[:, 0:F], T.acc1[:, 0:F], T.y_sb[:]]
+    cur = terms[0]
+    if waits[0] is not None:
+        ve.wait_ge(sem["arr_" + waits[0]], arrival(waits[0]))
+    for n in range(3):
+        ve.wait_ge(sem["arr_" + waits[n + 1]], arrival(waits[n + 1]))
+        if n > 0:
+            ve.wait_ge(sem.vs, n)
+        ve.tensor_tensor(outs[n], cur, terms[n + 1], AluOpType.add).then_inc(sem.fin if n == 2 else sem.vs, 1)
+        cur = outs[n]
+
+    g.sync.wait_ge(sem.fin, 1)
+    g.sync.dma_start(T.y[:], T.y_sb[:]).then_inc(sem.st, 16)
+    g.sync.wait_ge(sem.st, 16)
+    g.wait_ge(sem.sent, sent[0])

@@ -3,25 +3,28 @@ from concourse.mybir import AluOpType
 
 F = 256
 KINDS = ["far", "mate", "plane", "own"]
+ADD_ORDER = ["plane", "far", "mate"]
+AW = 5 * 128
 
 SCRATCH = {
     "a_sb": ("sbuf", [128, 2048], "bfloat16"),
     "w_sb": ("sbuf", [128, F], "bfloat16"),
     "w_in": ("sbuf", [128, 3 * F], "bfloat16"),
-    "a_in": ("sbuf", [128, 3 * 2 * F], "bfloat16"),
+    "a_in": ("sbuf", [128, 3 * AW], "bfloat16"),
     "out_sb": ("sbuf", [128, 4 * F], "bfloat16"),
-    "rx": ("sbuf", [128, 4 * F], "bfloat16"),
+    "rx": ("sbuf", [128, 3 * F], "bfloat16"),
     "y_sb": ("sbuf", [128, F], "bfloat16"),
     "ps0": ("psum", [128, 512], "float32"),
     "ps1": ("psum", [128, 512], "float32"),
     "ps2": ("psum", [128, 512], "float32"),
     "ps3": ("psum", [128, 512], "float32"),
+    "ps4": ("psum", [128, 512], "float32"),
     "acc0": ("psum", [128, 512], "float32"),
     "acc1": ("psum", [128, 512], "float32"),
 }
-SEMAPHORES = ["ld_far", "ld_mate", "ld_plane", "ld_own", "in1", "in2",
-              "mm0", "mm1", "mm2", "mm3", "cp0", "cp1", "cp2", "cp3",
-              "arr_far", "arr_mate", "arr_plane", "arr_own", "vs", "fin", "st", "sent"]
+SEMAPHORES = ["ld_far", "ld_mate", "ld_plane", "ld_own", "in0", "in1", "in2",
+              "mm0", "mm1", "mm2", "mm3", "mm4", "cp0", "cp1", "cp2", "cp3",
+              "arr_far", "arr_mate", "arr_plane", "vs", "fin", "st", "sent"]
 
 
 def _bits(mask):
@@ -59,27 +62,25 @@ def rank_program(g, core, T, topo):
     def is_port(k):
         return all(topo.may_write(k, d) for d in cores if d != k)
 
-    def kinds_of(k):
-        return ("far", "mate") if is_port(k) else ("plane", "own")
-
-    def owners(k, kd):
-        return ranks_on(chip_of_kind(topo.chip(k), kd), topo.die(k))
+    def jobs(k):
+        kds = ("far", "mate") if is_port(k) else ("plane",)
+        return [(kd, ranks_on(chip_of_kind(topo.chip(k), kd), topo.die(k))) for kd in kds] + [("own", [k])]
 
     def reducer(c, kd, die):
-        return [k for k in ranks_on(c, die) if kd in kinds_of(k)][0]
+        return [k for k in ranks_on(c, die) if kd in [j[0] for j in jobs(k)]][0]
 
     def exchange(k):
         rest = [d for d in ranks_on(topo.chip(k)) if d != k]
         ports = [d for d in rest if is_port(d)]
         plain = [d for d in rest if not is_port(d)]
         if is_port(k):
-            calls = [[(ports[0], "w"), (ports[0], 0)],
-                     [(ports[0], 1), (plain[0], "w"), (plain[1], "w")],
-                     [(plain[0], 0), (plain[1], 0), (plain[0], 1), (plain[1], 1)]]
+            calls = [[(ports[0], "w"), (ports[0], 0), (plain[0], "w"), (plain[1], "w")],
+                     [(ports[0], 1), (plain[0], 0), (plain[1], 0)],
+                     [(ports[0], 2), (plain[0], 1), (plain[1], 1)]]
         else:
             calls = [[(ports[0], "w"), (ports[1], "w"), (ports[0], 0), (ports[1], 0)],
                      [(ports[0], 1), (ports[1], 1), (plain[0], "w"), (plain[0], 0)],
-                     [(plain[0], 1)]]
+                     [(plain[0], 1), (ports[0], 2), (ports[1], 2)]]
         out = []
         for call in calls:
             n = min(len(_bits(topo.mask(k, d))) for d, _ in call)
@@ -88,7 +89,7 @@ def rank_program(g, core, T, topo):
 
     chip = topo.chip(core)
     mine = ranks_on(chip)
-    my_kinds = kinds_of(core)
+    my_jobs = jobs(core)
     sent = [0]
 
     def issue(items):
@@ -120,7 +121,7 @@ def rank_program(g, core, T, topo):
     for n, kd in enumerate(KINDS):
         c0 = min(col(k) for k in ranks_on(chip_of_kind(chip, kd)))
         q = g.scalar if n % 2 == 0 else g.sync
-        q.dma_start(T.a_sb[:, c0:c0 + 2 * F], T.a[:, c0:c0 + 2 * F]).then_inc(sem["ld_" + kd], 16)
+        q.dma_start(T.a_sb[:, c0:c0 + 512], T.a[:, c0:c0 + 512]).then_inc(sem["ld_" + kd], 16)
 
     waited = set()
     for call in exchange(core):
@@ -128,86 +129,88 @@ def rank_program(g, core, T, topo):
         for d, what, e in call:
             slot = [k for k in mine if k != d].index(core)
             if what == "w":
-                need, sap, dap, rs = "far", T.w_sb[:], T.w_in[:, F * slot:F * slot + F], sem.in1
+                need, sap, dap, rs = "far", T.w_sb[:], T.w_in[:, F * slot:F * slot + F], sem.in0
             else:
-                need = kinds_of(d)[what]
-                c0 = min(col(o) for o in owners(d, need))
-                sap = T.a_sb[:, c0:c0 + F]
-                dap = T.a_in[:, 2 * F * slot + F * what:2 * F * slot + F * what + F]
-                rs = sem.in1 if what == 0 else sem.in2
+                jd = jobs(d)
+                need, own = jd[what]
+                c0, wd = min(col(o) for o in own), 128 * len(own)
+                off = AW * slot + 128 * sum(len(j[1]) for j in jd[:what])
+                sap, dap, rs = T.a_sb[:, c0:c0 + wd], T.a_in[:, off:off + wd], sem["in%d" % what]
             if need not in waited:
                 waited.add(need)
                 g.wait_ge(sem["ld_" + need], ld_total[need])
             items.append((d, dap, sap, rs, e))
         issue(items)
 
-    in_total = [0, 0]
+    in_total = [0, 0, 0]
     for k in mine:
         if k != core:
             for call in exchange(k):
                 for d, what, e in call:
                     if d == core:
-                        in_total[1 if what == 1 else 0] += e
+                        in_total[0 if what == "w" else what] += e
 
-    blocks = [o for kd in my_kinds for o in owners(core, kd)]
-    ps = [T.ps0, T.ps1, T.ps2, T.ps3]
+    ps = [T.ps0, T.ps1, T.ps2, T.ps3, T.ps4]
     te = g.tensor
     te.wait_ge(sem.ld_far, ld_total["far"])
-    for kd in my_kinds:
+    first = {}
+    b = 0
+    for q, (kd, own) in enumerate(my_jobs):
+        first[q] = b
+        b += len(own)
+
+    def open_groups(q):
+        kd, own = my_jobs[q]
         if kd != "far":
             te.wait_ge(sem["ld_" + kd], ld_total[kd])
-    for b, o in enumerate(blocks):
-        te.matmul(ps[b][:, 0:F], T.a_sb[:, col(o):col(o) + 128], T.w_sb[:], True, False)
-    for half in range(2):
-        te.wait_ge(sem.in1 if half == 0 else sem.in2, in_total[half])
-        for b in (2 * half, 2 * half + 1):
+        for n, o in enumerate(own):
+            te.matmul(ps[first[q] + n][:, 0:F], T.a_sb[:, col(o):col(o) + 128], T.w_sb[:], True, False)
+
+    for q, (kd, own) in enumerate(my_jobs):
+        if kd != "own":
+            open_groups(q)
+    for q, (kd, own) in enumerate(my_jobs):
+        if kd == "own":
+            open_groups(q)
+        te.wait_ge(sem["in%d" % q], in_total[q])
+        for n in range(len(own)):
+            b = first[q] + n
             for s in range(3):
-                mm = te.matmul(ps[b][:, 0:F], T.a_in[:, 2 * F * s + 128 * b:2 * F * s + 128 * b + 128],
+                mm = te.matmul(ps[b][:, 0:F], T.a_in[:, AW * s + 128 * b:AW * s + 128 * b + 128],
                                T.w_in[:, F * s:F * s + F], False, s == 2)
             mm.then_inc(sem["mm%d" % b], 1)
 
     ve = g.vector
-    for b, o in enumerate(blocks):
-        if o != core:
-            ve.wait_ge(sem["mm%d" % b], 1)
-            ve.tensor_copy(T.out_sb[:, F * b:F * b + F], ps[b][:, 0:F]).then_inc(sem["cp%d" % b], 1)
-    for half, kd in enumerate(my_kinds):
+    for q, (kd, own) in enumerate(my_jobs):
+        if kd == "own":
+            continue
         slot = KINDS.index(kd)
         items = []
-        todo = [b for b in (2 * half, 2 * half + 1) if blocks[b] != core]
-        for b in todo:
+        for n, o in enumerate(own):
+            b = first[q] + n
+            ve.wait_ge(sem["mm%d" % b], 1)
+            ve.tensor_copy(T.out_sb[:, F * b:F * b + F], ps[b][:, 0:F]).then_inc(sem["cp%d" % b], 1)
             g.wait_ge(sem["cp%d" % b], 1)
-            e = len(_bits(topo.mask(core, blocks[b]))) // len(todo)
-            items.append((blocks[b], T.rx[:, F * slot:F * slot + F], T.out_sb[:, F * b:F * b + F],
-                          sem["arr_" + kd], e))
+            items.append((o, T.rx[:, F * slot:F * slot + F], T.out_sb[:, F * b:F * b + F], sem["arr_" + kd],
+                          len(_bits(topo.mask(core, o))) // len(own)))
         issue(items)
 
     def arrival(kd):
         s = reducer(chip_of_kind(chip, kd), kd, topo.die(core))
-        n = len([o for o in owners(s, kd) if o != s])
+        n = [len(j[1]) for j in jobs(s) if j[0] == kd][0]
         return len(_bits(topo.mask(s, core))) // n
 
-    def rx(kd):
-        slot = KINDS.index(kd)
-        return T.rx[:, F * slot:F * slot + F]
-
-    if core in blocks:
-        b = blocks.index(core)
-        ve.wait_ge(sem["mm%d" % b], 1)
-        terms = [ps[b][:, 0:F]] + [rx(kd) for kd in ("far", "mate", "plane")]
-        waits = [None, "far", "mate", "plane"]
-    else:
-        terms = [rx(kd) for kd in KINDS]
-        waits = list(KINDS)
+    b = first[len(my_jobs) - 1]
+    ve.wait_ge(sem["mm%d" % b], 1)
+    cur = ps[b][:, 0:F]
     outs = [T.acc0[:, 0:F], T.acc1[:, 0:F], T.y_sb[:]]
-    cur = terms[0]
-    if waits[0] is not None:
-        ve.wait_ge(sem["arr_" + waits[0]], arrival(waits[0]))
-    for n in range(3):
-        ve.wait_ge(sem["arr_" + waits[n + 1]], arrival(waits[n + 1]))
+    for n, kd in enumerate(ADD_ORDER):
+        slot = KINDS.index(kd)
+        ve.wait_ge(sem["arr_" + kd], arrival(kd))
         if n > 0:
             ve.wait_ge(sem.vs, n)
-        ve.tensor_tensor(outs[n], cur, terms[n + 1], AluOpType.add).then_inc(sem.fin if n == 2 else sem.vs, 1)
+        ve.tensor_tensor(outs[n], cur, T.rx[:, F * slot:F * slot + F],
+                         AluOpType.add).then_inc(sem.fin if n == 2 else sem.vs, 1)
         cur = outs[n]
 
     g.sync.wait_ge(sem.fin, 1)

@@ -3,7 +3,8 @@ from concourse.mybir import AluOpType
 
 F = 256
 KINDS = ["far", "mate", "plane", "own"]
-ADD_ORDER = ["plane", "far", "mate"]
+ADD_ORDER = ["plane", "mate", "far"]
+ALONE = ["far"]
 AW = 5 * 128
 
 SCRATCH = {
@@ -185,6 +186,7 @@ def rank_program(g, core, T, topo):
         if kd == "own":
             continue
         slot = KINDS.index(kd)
+        together = 1 if kd in ALONE else len(own)
         items = []
         for n, o in enumerate(own):
             b = first[q] + n
@@ -192,12 +194,14 @@ def rank_program(g, core, T, topo):
             ve.tensor_copy(T.out_sb[:, F * b:F * b + F], ps[b][:, 0:F]).then_inc(sem["cp%d" % b], 1)
             g.wait_ge(sem["cp%d" % b], 1)
             items.append((o, T.rx[:, F * slot:F * slot + F], T.out_sb[:, F * b:F * b + F], sem["arr_" + kd],
-                          len(_bits(topo.mask(core, o))) // len(own)))
-        issue(items)
+                          len(_bits(topo.mask(core, o))) // together))
+            if len(items) == together:
+                issue(items)
+                items = []
 
     def arrival(kd):
         s = reducer(chip_of_kind(chip, kd), kd, topo.die(core))
-        n = [len(j[1]) for j in jobs(s) if j[0] == kd][0]
+        n = 1 if kd in ALONE else [len(j[1]) for j in jobs(s) if j[0] == kd][0]
         return len(_bits(topo.mask(s, core))) // n
 
     b = first[len(my_jobs) - 1]

from concourse.bass import DstId, RemoteDMATransfer
from concourse.mybir import AluOpType

F = 256
KINDS = ["far", "mate", "plane", "own"]
ADD_ORDER = ["plane", "mate", "far"]
ALONE = ["far"]
AW = 5 * 128

SCRATCH = {
    "a_sb": ("sbuf", [128, 2048], "bfloat16"),
    "w_sb": ("sbuf", [128, F], "bfloat16"),
    "w_in": ("sbuf", [128, 3 * F], "bfloat16"),
    "a_in": ("sbuf", [128, 3 * AW], "bfloat16"),
    "out_sb": ("sbuf", [128, 4 * F], "bfloat16"),
    "rx": ("sbuf", [128, 3 * F], "bfloat16"),
    "y_sb": ("sbuf", [128, F], "bfloat16"),
    "ps0": ("psum", [128, 512], "float32"),
    "ps1": ("psum", [128, 512], "float32"),
    "ps2": ("psum", [128, 512], "float32"),
    "ps3": ("psum", [128, 512], "float32"),
    "ps4": ("psum", [128, 512], "float32"),
    "acc0": ("psum", [128, 512], "float32"),
    "acc1": ("psum", [128, 512], "float32"),
}
SEMAPHORES = ["ld_far", "ld_mate", "ld_plane", "ld_own", "in0", "in1", "in2",
              "mm0", "mm1", "mm2", "mm3", "mm4", "cp0", "cp1", "cp2", "cp3",
              "arr_far", "arr_mate", "arr_plane", "vs", "fin", "st", "sent"]


def _bits(mask):
    return [1 << b for b in range(mask.bit_length()) if (mask >> b) & 1]


def _shares(n_items, n_engines):
    if n_items == 3:
        return [n_engines // 2, n_engines // 4, n_engines // 4]
    return [n_engines // n_items] * n_items


def rank_program(g, core, T, topo):
    if T.rank_of(core) is None:
        return
    cores = list(T.cores)
    sem = T.sem
    chips = sorted({topo.chip(k) for k in cores})

    def kind(c, x):
        if x == c:
            return "own"
        if topo.mates(c, x):
            return "mate"
        if topo.same_plane(c, x):
            return "plane"
        return "far"

    def chip_of_kind(c, kd):
        return [x for x in chips if kind(c, x) == kd][0]

    def ranks_on(c, die=None):
        return [k for k in cores if topo.chip(k) == c and (die is None or topo.die(k) == die)]

    def is_port(k):
        return all(topo.may_write(k, d) for d in cores if d != k)

    def jobs(k):
        kds = ("far", "mate") if is_port(k) else ("plane",)
        return [(kd, ranks_on(chip_of_kind(topo.chip(k), kd), topo.die(k))) for kd in kds] + [("own", [k])]

    def reducer(c, kd, die):
        return [k for k in ranks_on(c, die) if kd in [j[0] for j in jobs(k)]][0]

    def exchange(k):
        rest = [d for d in ranks_on(topo.chip(k)) if d != k]
        ports = [d for d in rest if is_port(d)]
        plain = [d for d in rest if not is_port(d)]
        if is_port(k):
            calls = [[(ports[0], "w"), (ports[0], 0), (plain[0], "w"), (plain[1], "w")],
                     [(ports[0], 1), (plain[0], 0), (plain[1], 0)],
                     [(ports[0], 2), (plain[0], 1), (plain[1], 1)]]
        else:
            calls = [[(ports[0], "w"), (ports[1], "w"), (ports[0], 0), (ports[1], 0)],
                     [(ports[0], 1), (ports[1], 1), (plain[0], "w"), (plain[0], 0)],
                     [(plain[0], 1), (ports[0], 2), (ports[1], 2)]]
        out = []
        for call in calls:
            n = min(len(_bits(topo.mask(k, d))) for d, _ in call)
            out.append([(d, what, e) for (d, what), e in zip(call, _shares(len(call), n))])
        return out

    chip = topo.chip(core)
    mine = ranks_on(chip)
    my_jobs = jobs(core)
    sent = [0]

    def issue(items):
        pool = None
        for d, _, _, _, _ in items:
            m = topo.mask(core, d)
            pool = m if pool is None else pool & m
        pool = _bits(pool)
        trs, i = [], 0
        for d, dap, sap, rs, e in items:
            rid, pid, _ = topo.addr(d)
            trs.append((rid, pid, sum(pool[i:i + e]), dap, sap, rs))
            i += e
            sent[0] += e
        if len(trs) == 1:
            rid, pid, m, dap, sap, rs = trs[0]
            g.remote_dma(dap, sap, rs, sem.sent, pid, rid, m)
        else:
            g.remote_dma_fused([RemoteDMATransfer(dst_ids=[DstId(rid=rid, pnc=pid)], dma_engine_mask=m,
                                                  remote_sem=rs, src=sap, dst=dap)
                                for rid, pid, m, dap, sap, rs in trs], local_sem=sem.sent)

    def col(k):
        return 128 * T.rank_of(k)

    ld_total = {kd: 16 for kd in KINDS}
    ld_total["far"] = 32
    g.sync.dma_start(T.w_sb[:], T.w[:]).then_inc(sem.ld_far, 16)
    for n, kd in enumerate(KINDS):
        c0 = min(col(k) for k in ranks_on(chip_of_kind(chip, kd)))
        q = g.scalar if n % 2 == 0 else g.sync
        q.dma_start(T.a_sb[:, c0:c0 + 512], T.a[:, c0:c0 + 512]).then_inc(sem["ld_" + kd], 16)

    waited = set()
    for call in exchange(core):
        items = []
        for d, what, e in call:
            slot = [k for k in mine if k != d].index(core)
            if what == "w":
                need, sap, dap, rs = "far", T.w_sb[:], T.w_in[:, F * slot:F * slot + F], sem.in0
            else:
                jd = jobs(d)
                need, own = jd[what]
                c0, wd = min(col(o) for o in own), 128 * len(own)
                off = AW * slot + 128 * sum(len(j[1]) for j in jd[:what])
                sap, dap, rs = T.a_sb[:, c0:c0 + wd], T.a_in[:, off:off + wd], sem["in%d" % what]
            if need not in waited:
                waited.add(need)
                g.wait_ge(sem["ld_" + need], ld_total[need])
            items.append((d, dap, sap, rs, e))
        issue(items)

    in_total = [0, 0, 0]
    for k in mine:
        if k != core:
            for call in exchange(k):
                for d, what, e in call:
                    if d == core:
                        in_total[0 if what == "w" else what] += e

    ps = [T.ps0, T.ps1, T.ps2, T.ps3, T.ps4]
    te = g.tensor
    te.wait_ge(sem.ld_far, ld_total["far"])
    first = {}
    b = 0
    for q, (kd, own) in enumerate(my_jobs):
        first[q] = b
        b += len(own)

    def open_groups(q):
        kd, own = my_jobs[q]
        if kd != "far":
            te.wait_ge(sem["ld_" + kd], ld_total[kd])
        for n, o in enumerate(own):
            te.matmul(ps[first[q] + n][:, 0:F], T.a_sb[:, col(o):col(o) + 128], T.w_sb[:], True, False)

    for q, (kd, own) in enumerate(my_jobs):
        if kd != "own":
            open_groups(q)
    for q, (kd, own) in enumerate(my_jobs):
        if kd == "own":
            open_groups(q)
        te.wait_ge(sem["in%d" % q], in_total[q])
        for n in range(len(own)):
            b = first[q] + n
            for s in range(3):
                mm = te.matmul(ps[b][:, 0:F], T.a_in[:, AW * s + 128 * b:AW * s + 128 * b + 128],
                               T.w_in[:, F * s:F * s + F], False, s == 2)
            mm.then_inc(sem["mm%d" % b], 1)

    ve = g.vector
    for q, (kd, own) in enumerate(my_jobs):
        if kd == "own":
            continue
        slot = KINDS.index(kd)
        together = 1 if kd in ALONE else len(own)
        items = []
        for n, o in enumerate(own):
            b = first[q] + n
            ve.wait_ge(sem["mm%d" % b], 1)
            ve.tensor_copy(T.out_sb[:, F * b:F * b + F], ps[b][:, 0:F]).then_inc(sem["cp%d" % b], 1)
            g.wait_ge(sem["cp%d" % b], 1)
            items.append((o, T.rx[:, F * slot:F * slot + F], T.out_sb[:, F * b:F * b + F], sem["arr_" + kd],
                          len(_bits(topo.mask(core, o))) // together))
            if len(items) == together:
                issue(items)
                items = []

    def arrival(kd):
        s = reducer(chip_of_kind(chip, kd), kd, topo.die(core))
        n = 1 if kd in ALONE else [len(j[1]) for j in jobs(s) if j[0] == kd][0]
        return len(_bits(topo.mask(s, core))) // n

    b = first[len(my_jobs) - 1]
    ve.wait_ge(sem["mm%d" % b], 1)
    cur = ps[b][:, 0:F]
    outs = [T.acc0[:, 0:F], T.acc1[:, 0:F], T.y_sb[:]]
    for n, kd in enumerate(ADD_ORDER):
        slot = KINDS.index(kd)
        ve.wait_ge(sem["arr_" + kd], arrival(kd))
        if n > 0:
            ve.wait_ge(sem.vs, n)
        ve.tensor_tensor(outs[n], cur, T.rx[:, F * slot:F * slot + F],
                         AluOpType.add).then_inc(sem.fin if n == 2 else sem.vs, 1)
        cur = outs[n]

    g.sync.wait_ge(sem.fin, 1)
    g.sync.dma_start(T.y[:], T.y_sb[:]).then_inc(sem.st, 16)
    g.sync.wait_ge(sem.st, 16)
    g.wait_ge(sem.sent, sent[0])
